import numpy as np
import ml_dtypes


def mxq(x, axis, fmt="e4m3"):
    dtype, down = {"e4m3": (ml_dtypes.float8_e4m3fn, 7), "e5m2": (ml_dtypes.float8_e5m2, 14)}[fmt]
    v = np.moveaxis(np.asarray(x, np.float32).astype(ml_dtypes.bfloat16).astype(np.float64), axis, -1)
    blocks = v.reshape(v.shape[:-1] + (-1, 32))
    amax = np.abs(blocks).max(-1, keepdims=True)
    byte = np.maximum(np.where(amax > 0, np.frexp(amax)[1] - 1 + 127, 0) - down, 1)
    scale = np.exp2(byte - 127.0)
    codes = (blocks / scale).astype(np.float32).astype(dtype).astype(np.float64)
    return np.moveaxis((codes * scale).reshape(v.shape), -1, axis)


WIDE = False


def mx_kscale(k):
    if not WIDE:
        return np.ones(k)
    levels = np.array([10, -10, 5, -5, 0])
    if k % 512:
        return np.exp2(np.random.permutation(np.resize(levels, k // 32))).repeat(32)
    a = np.empty((k // 512, 16))
    for p in range(k // 512):
        a[p, :8] = np.random.permutation(np.resize(levels, 8))
        for g in range(8):
            far = levels[np.abs(levels - a[p, g]) >= 10]
            a[p, g + 8] = far[np.random.randint(len(far))]
    return np.exp2(a.ravel()).repeat(32)


BF16 = ml_dtypes.bfloat16


def bf(x):
    return np.asarray(x, np.float32).astype(BF16)


def f64(x):
    return np.asarray(x).astype(np.float64)


M, T, D, F = 3, 1024, 1024, 512

SHRINK = 0.8
STEP = 0.3


def shrink_scale(d, t):
    idx = np.arange(d)
    on_diag = idx[:, None] == idx[None, :]
    return np.where(on_diag, 1.0 / t, SHRINK / t)


def draw0():
    a, b = mx_kscale(T), mx_kscale(D)
    return {"x": bf(np.random.standard_normal((M, T, D))),
            "u": bf((1.0 + 0.1 * np.random.standard_normal((M, T))) * a),
            "v": bf((1.0 + 0.1 * np.random.standard_normal((M, T))) / a),
            "c": bf((1.0 + 0.1 * np.random.standard_normal((M, D))) * b),
            "tau": bf(np.random.standard_normal((M, D, F)) / b[:, None]),
            "w0": bf(np.random.standard_normal((D, F)))}


def core(x, u, v, c, tau, w0):
    x, u, v, c, tau, w0 = f64(x), f64(u), f64(v), f64(c), f64(tau), f64(w0)
    t = x.shape[1]
    d = x.shape[2]
    xu = mxq(u[:, :, None] * x, 1, "e4m3")
    xv = mxq(v[:, :, None] * x, 1, "e4m3")
    gram = xu.transpose(0, 2, 1) @ xv
    s = gram * shrink_scale(d, t)[None, :, :]
    p = s * c[:, None, :]
    r = mxq(p, 2, "e4m3") @ mxq(tau, 1, "e4m3")
    return w0 + STEP * np.sum(r, axis=0)


def e4m3fn_bytes(y):
    return np.clip(np.asarray(y, np.float64), -448.0, 448.0).astype(np.float32).astype(ml_dtypes.float8_e4m3fn).view(np.uint8)


def e4m3fn_values(b):
    return np.asarray(b, np.uint8).view(ml_dtypes.float8_e4m3fn).astype(np.float64)


def setup_inputs():
    d = draw0()
    x0 = np.asarray(d['tau']).astype(np.float64)
    s = (np.max(np.abs(x0), axis=(0, 2), keepdims=True) / 448.0).astype(np.float32)
    out = {}
    for k, v in d.items():
        if k == 'tau':
            out['tau_bytes'] = e4m3fn_bytes(x0 / s.astype(np.float64))
            out['tau_scale'] = s
        else:
            out[k] = v
    return out


def reference(x, u, v, c, tau_bytes, tau_scale, w0):
    return core(x, u, v, c, e4m3fn_values(tau_bytes) * tau_scale.astype(np.float64), w0)

@@ -1,0 +1,346 @@
+from contextlib import ExitStack
+
+import concourse.mybir as mybir
+from concourse.masks import make_identity
+
+M, T, D, F = 3, 1024, 1024, 512
+SHRINK, STEP = 0.8, 0.3
+
+FLOPS = M * (2 * D * D * T + 2 * D * D * F)
+
+P = 128
+PACK = 4
+KP = P * PACK
+NG = T // KP
+H = 512
+
+F32 = mybir.dt.float32
+BF16 = mybir.dt.bfloat16
+U32 = mybir.dt.uint32
+U8 = mybir.dt.uint8
+E4 = mybir.dt.float8_e4m3fn
+X4 = mybir.dt.float8_e4m3fn_x4
+ALU = mybir.AluOpType
+COPY = mybir.ActivationFunctionType.Copy
+
+TV = ((0, 0), (0, 1), (1, 0), (1, 1))
+PS = ()
+UNITS = [(m, gp, g) for m in range(M - 1) for (gp, g) in ((0, 0), (0, 1), (1, 0), (1, 1))] + [
+    (M - 1, 0, 0), (M - 1, 0, 1), (M - 1, 1, 1), (M - 1, 1, 0)]
+CHUNKS = [(m, h) for m in range(M) for h in range(2)]
+
+
+def tile_regmeangramdescentmerge_kernel(tc, x, u, v, c, tau_bytes, tau_scale, w0, out):
+    nc = tc.nc
+    with ExitStack() as ctx:
+        pool = ctx.enter_context(tc.tile_pool(name="sb", bufs=1))
+        psum = ctx.enter_context(tc.psum_pool(name="ps", bufs=4))
+
+        ident = pool.tile([P, P], BF16, name="ident")
+        boost = pool.tile([P, P], F32, name="boost")
+        rows = pool.tile([P, KP], BF16, name="rows")
+        gains = pool.tile([P, 12, PACK], BF16, name="gains")
+        cs = pool.tile([P, 6, PACK], F32, name="cs")
+        ts = pool.tile([P, NG, PACK], F32, name="ts")
+        w0_sb = pool.tile([P, 2, PACK, F], BF16, name="w0_sb")
+
+        raw, xi, cu, cv, tb, tcod, pcod, banks, planes, pmix, prod, tmix = ({} for _ in range(12))
+        obank, tpl, dg, pbank = {}, {}, {}, {}
+        ocount = {}
+
+        def load_x(m, h, g):
+            if g == 0:
+                r = pool.tile([P, NG, PACK, H], BF16, name="raw", bufs=5)
+                raw[m, h] = r
+            nc.sync.dma_start(
+                out=raw[m, h][:, g],
+                in_=x[m, g * KP:(g + 1) * KP, h * H:(h + 1) * H].rearrange("(p t) d -> p t d", t=PACK))
+
+        def load_tau(m):
+            b = pool.tile([P, NG, PACK, F], U8, name="tb", bufs=2)
+            tb[m] = b
+            nc.sync.dma_start(out=b[:].rearrange("p g t f -> p g (t f)"),
+                              in_=tau_bytes[m].rearrange("(g p t) f -> p g (t f)", p=P, t=PACK))
+
+        def inter(eng, m, h, g, lo=0, hi=H):
+            if lo == 0:
+                xt = pool.tile([P, H * PACK], BF16, name="xi", bufs=2, align_bytes=64)
+                xi[m, h] = xt
+            src = raw[m, h][:, g, :, lo:hi].rearrange("p t (c i) -> p c t i", i=4)
+            dst = xi[m, h][:, lo * PACK:hi * PACK].rearrange("p (c i t) -> p c t i", i=4, t=PACK)
+            eng(out=dst, in_=src)
+
+        def gain(m, h, g, op):
+            if (m, h, op) not in prod:
+                pt = pool.tile([P, NG, H * PACK], BF16, name="prod", bufs=4, align_bytes=64)
+                prod[m, h, op] = pt
+            col = 6 * op + 2 * m + g
+            nc.vector.tensor_tensor(
+                out=prod[m, h, op][:, g].rearrange("p (b n t) -> p b n t", b=PACK, t=PACK),
+                in0=xi[m, h][:].rearrange("p (n b t) -> p b n t", b=PACK, t=PACK),
+                in1=gains[:, col].unsqueeze(1).unsqueeze(1).broadcast_to([P, PACK, P, PACK]),
+                op=ALU.mult)
+
+        def diags(eng, m):
+            for op in range(2):
+                for t in range(PACK):
+                    dt_ = pool.tile([P, P], BF16, name="dg", bufs=24)
+                    dg[m, op, t] = dt_
+                    eng.tensor_scalar(out=dt_[:], in0=ident[:], scalar1=gains[:, 6 * op + 2 * m + 1, t:t + 1], scalar2=None, op0=ALU.mult)
+
+        def pmm(m, h, op):
+            if (m, h, op) not in prod:
+                pt = pool.tile([P, NG, H * PACK], BF16, name="prod", bufs=4, align_bytes=64)
+                prod[m, h, op] = pt
+            for b in range(PACK):
+                bank = psum.tile([P, PACK, P], F32, name="ob")
+                pbank[m, h, op, b] = bank
+                for t in range(PACK):
+                    nc.tensor.matmul(out=bank[:, t], lhsT=dg[m, op, t][:], rhs=raw[m, h][:, 1, t, b:H:PACK], start=True, stop=True)
+
+        def pev(m, h, op, b):
+            nc.scalar.copy(out=prod[m, h, op][:, 1, b * H:(b + 1) * H].rearrange("p (n t) -> p n t", t=PACK),
+                           in_=pbank[m, h, op, b][:].rearrange("p t n -> p n t"))
+
+        def quant_x(m, h, op):
+            if op == 0:
+                cod = pool.tile([P, NG, H], U32, name="cu", bufs=4, align_bytes=64)
+                sca = pool.tile([P, NG, H], U8, name="cus", bufs=4, align_bytes=64)
+                cu[m, h] = (cod, sca)
+            else:
+                cod = pool.tile([P, NG, H], U32, name="cv", bufs=4, align_bytes=64)
+                sca = pool.tile([P, NG, H], U8, name="cvs", bufs=4, align_bytes=64)
+                cv[m, h] = (cod, sca)
+            nc.vector.quantize_mx(
+                out=cod[:].rearrange("p g d -> p (g d)").bitcast(X4),
+                scales=sca[:].rearrange("p g d -> p (g d)"),
+                in_=prod[m, h, op][:].rearrange("p g d -> p (g d)"))
+
+        def widen(m, g):
+            tp = pool.tile([P, PACK, F], BF16, name="tp", bufs=2)
+            for t in range(PACK):
+                nc.scalar.activation(out=tp[:, t], in_=tb[m][:, g, t].bitcast(E4), func=COPY, scale=ts[:, g, t:t + 1])
+            tpl[m, g] = tp
+
+        def tint(m, g):
+            tm = pool.tile([P, F * PACK], BF16, name="tm", bufs=2, align_bytes=64)
+            tmix[m, g] = tm
+            eng = nc.vector.tensor_copy if (m, g) in TV else nc.scalar.copy
+            eng(out=tm[:].rearrange("p (c i t) -> p c t i", i=4, t=PACK),
+                in_=tpl[m, g][:].rearrange("p t (c i) -> p c t i", i=4))
+
+        def quant_tau(m, g):
+            cod = pool.tile([P, F], U32, name="tc", bufs=6, align_bytes=64)
+            sca = pool.tile([P, F], U8, name="tcs", bufs=6, align_bytes=64)
+            tcod[m, g] = (cod, sca)
+            nc.vector.quantize_mx(out=cod[:].bitcast(X4), scales=sca[:], in_=tmix[m, g][:])
+
+        def gram(un):
+            m, gp, g = un
+            banks[un] = []
+            for t in range(PACK):
+                bank = psum.tile([P, H], F32, name="gr")
+                banks[un].append(bank)
+                for k in range(NG):
+                    nc.tensor.matmul_mx(
+                        out=bank[:],
+                        lhsT=cv[m, g][0][:, k, t * P:(t + 1) * P].bitcast(X4),
+                        lhsT_scale=cv[m, g][1][:, k, t * P:(t + 1) * P],
+                        rhs=cu[m, gp][0][:, k].bitcast(X4),
+                        rhs_scale=cu[m, gp][1][:, k],
+                        start=(k == 0), stop=(k == NG - 1))
+
+        def evac(un, t):
+            m, gp, g = un
+            if un not in planes:
+                pl = pool.tile([P, PACK, H], BF16, name="pl", bufs=2)
+                planes[un] = pl
+            parts = [(0, H)] if gp != g else [(a, b) for (a, b) in ((0, t * P), ((t + 1) * P, H)) if b > a]
+            for a, b in parts:
+                nc.scalar.activation(out=planes[un][:, t, a:b], in_=banks[un][t][:, a:b], func=COPY,
+                                     scale=cs[:, 2 * m + g, t:t + 1])
+
+        def diag(un, t):
+            m, gp, g = un
+            if t == 0:
+                pl = pool.tile([P, PACK, H], BF16, name="pl", bufs=2)
+                planes[un] = pl
+            if gp == g:
+                win = slice(t * P, (t + 1) * P)
+                nc.vector.scalar_tensor_tensor(
+                    out=planes[un][:, t, win], in0=banks[un][t][:, win], scalar=cs[:, 2 * m + g, t:t + 1],
+                    in1=boost[:], op0=ALU.mult, op1=ALU.mult)
+
+        def pint(un):
+            pm = pool.tile([P, H * PACK], BF16, name="pm", bufs=2, align_bytes=64)
+            pmix[un] = pm
+            eng = nc.scalar.copy if UNITS.index(un) in PS else nc.vector.tensor_copy
+            eng(out=pm[:].rearrange("p (c i t) -> p c t i", i=4, t=PACK),
+                                  in_=planes[un][:].rearrange("p t (c i) -> p c t i", i=4))
+
+        def quant_p(un):
+            cod = pool.tile([P, H], U32, name="pc", bufs=12, align_bytes=64)
+            sca = pool.tile([P, H], U8, name="pcs", bufs=12, align_bytes=64)
+            pcod[un] = (cod, sca)
+            nc.vector.quantize_mx(out=cod[:].bitcast(X4), scales=sca[:], in_=pmix[un][:])
+
+        def apply(un):
+            m, gp, g = un
+            for b in range(PACK):
+                if (gp, b) not in obank:
+                    ob = psum.tile([P, F], F32, name="ob")
+                    obank[gp, b] = ob
+                    ocount[gp, b] = 0
+                n = ocount[gp, b]
+                nc.tensor.matmul_mx(
+                    out=obank[gp, b][:],
+                    lhsT=pcod[un][0][:, b * P:(b + 1) * P].bitcast(X4),
+                    lhsT_scale=pcod[un][1][:, b * P:(b + 1) * P],
+                    rhs=tcod[m, g][0][:].bitcast(X4),
+                    rhs_scale=tcod[m, g][1][:],
+                    start=(n == 0), stop=(n == 2 * M - 1))
+                ocount[gp, b] = n + 1
+
+        def apply_all(half, last):
+            for un in UNITS:
+                if un[1] == half and (UNITS.index(un) <= UNITS.index(last)):
+                    apply(un)
+
+        def finish(gp, b):
+            o = pool.tile([P, F], F32, name="o", bufs=4)
+            nc.vector.scalar_tensor_tensor(out=o[:], in0=obank[gp, b][:], scalar=STEP, in1=w0_sb[:, gp, b],
+                                           op0=ALU.mult, op1=ALU.add)
+            nc.sync.dma_start(out=out.rearrange("(g p b) f -> g b p f", g=2, b=PACK)[gp, b], in_=o[:])
+
+
+        nc.vector.memset(rows[:], 0.0)
+        for i, src in enumerate((u, v, c)):
+            nc.scalar.dma_start(out=rows[6 * i:6 * i + 6, :], in_=src.rearrange("m (g k) -> (m g) k", g=NG))
+        load_x(0, 0, 0)
+        load_x(0, 0, 1)
+        nc.scalar.dma_start(out=ts[:], in_=tau_scale.rearrange("o (g p t) z -> p (o g) (t z)", p=P, t=PACK))
+        load_x(0, 1, 0)
+        load_x(0, 1, 1)
+        load_tau(0)
+        load_x(1, 0, 0)
+        load_x(1, 0, 1)
+        load_x(1, 1, 0)
+        load_x(1, 1, 1)
+        load_tau(1)
+        load_x(2, 0, 0)
+        load_x(2, 0, 1)
+        nc.sync.dma_start(out=w0_sb[:].rearrange("p g b f -> p g (b f)"),
+                          in_=w0.rearrange("(g p b) f -> p g (b f)", g=2, b=PACK))
+        make_identity(nc, ident[:])
+
+        tg = psum.tile([P, PACK, P], BF16, name="gr")
+        for t in range(PACK):
+            nc.tensor.transpose(tg[:, t], rows[:, t:KP:PACK], ident[:])
+        nc.vector.tensor_copy(out=gains[:], in_=tg[:, :, 0:12].rearrange("p t r -> p r t"))
+        diags(nc.vector, 0)
+        nc.vector.tensor_scalar(out=cs[:], in0=tg[:, :, 12:18].rearrange("p t r -> p r t"), scalar1=SHRINK / T,
+                                scalar2=None, op0=ALU.mult)
+        nc.vector.tensor_scalar(out=boost[:], in0=ident[:], scalar1=0.25, scalar2=1.0, op0=ALU.mult, op1=ALU.add)
+        diags(nc.vector, 1)
+        diags(nc.vector, 2)
+
+        pmm(0, 0, 0)
+        inter(nc.vector.tensor_copy, 0, 0, 0)
+        for b in range(PACK):
+            pev(0, 0, 0, b)
+        gain(0, 0, 0, 0)
+        pmm(0, 0, 1)
+        for b in range(PACK):
+            pev(0, 0, 1, b)
+        gain(0, 0, 0, 1)
+        inter(nc.vector.tensor_copy, 0, 1, 0)
+        quant_x(0, 0, 0)
+        gain(0, 1, 0, 0)
+        quant_x(0, 0, 1)
+        pmm(0, 1, 0)
+        for b in range(PACK):
+            pev(0, 1, 0, b)
+        gram(UNITS[0])
+        pmm(0, 1, 1)
+        for b in range(PACK):
+            pev(0, 1, 1, b)
+
+        plan = {1: UNITS[0:1], 2: UNITS[1:3], 3: UNITS[3:5], 4: UNITS[5:7], 5: UNITS[7:9]}
+        for k in range(1, 6):
+            m, h = CHUNKS[k]
+            todo = plan[k]
+            nxt = CHUNKS[k + 1] if k < 5 else None
+            if k == 3:
+                load_tau(2)
+            if k == 2:
+                load_x(2, 1, 0)
+                load_x(2, 1, 1)
+            a = todo[0]
+            b = todo[1] if len(todo) > 1 else None
+            jt = ((k - 1) // 2, (k - 1) % 2)
+            gain(m, h, 0, 1)
+            for t in range(PACK):
+                diag(a, t)
+                evac(a, t)
+            if nxt:
+                pmm(*nxt, 0)
+            if b:
+                gram(b)
+            quant_x(m, h, 0)
+            if nxt:
+                for w in range(PACK):
+                    pev(*nxt, 0, w)
+            pint(a)
+            quant_x(m, h, 1)
+            quant_p(a)
+            if nxt:
+                pmm(*nxt, 1)
+                inter(nc.vector.tensor_copy, *nxt, 0)
+            if b:
+                for t in range(PACK):
+                    diag(b, t)
+                    evac(b, t)
+            if nxt:
+                gain(*nxt, 0, 0)
+            gram(plan[k + 1][0] if k < 5 else UNITS[9])
+            widen(*jt)
+            if nxt:
+                for w in range(PACK):
+                    pev(*nxt, 1, w)
+            if b:
+                pint(b)
+                if k == 5:
+                    apply_all(0, UNITS[7])
+            tint(*jt)
+            if b:
+                quant_p(b)
+            quant_tau(*jt)
+            if k == 5:
+                widen(2, 1)
+
+        u9, u10, u11 = UNITS[9:12]
+        for t in range(PACK):
+            evac(u9, t)
+        gram(u10)
+        apply(UNITS[8])
+        tint(2, 1)
+        pint(u9)
+        quant_tau(2, 1)
+        for t in range(PACK):
+            diag(u10, t)
+            evac(u10, t)
+        quant_p(u9)
+        gram(u11)
+        apply(u9)
+        pint(u10)
+        for t in range(PACK):
+            evac(u11, t)
+        for b in range(PACK):
+            finish(0, b)
+        quant_p(u10)
+        pint(u11)
+        quant_p(u11)
+        apply_all(1, u10)
+        apply(u11)
+        for b in range(PACK):
+            finish(1, b)

@@ -23,7 +23,8 @@ X4 = mybir.dt.float8_e4m3fn_x4
 ALU = mybir.AluOpType
 COPY = mybir.ActivationFunctionType.Copy
 
-TV = ((0, 0), (0, 1), (1, 0), (1, 1))
+TV = ()
+TP = ()
 PS = ()
 UNITS = [(m, gp, g) for m in range(M - 1) for (gp, g) in ((0, 0), (0, 1), (1, 0), (1, 1))] + [
     (M - 1, 0, 0), (M - 1, 0, 1), (M - 1, 1, 1), (M - 1, 1, 0)]
@@ -44,8 +45,8 @@ def tile_regmeangramdescentmerge_kernel(tc, x, u, v, c, tau_bytes, tau_scale, w0
         ts = pool.tile([P, NG, PACK], F32, name="ts")
         w0_sb = pool.tile([P, 2, PACK, F], BF16, name="w0_sb")
 
-        raw, xi, cu, cv, tb, tcod, pcod, banks, planes, pmix, prod, tmix = ({} for _ in range(12))
-        obank, tpl, dg, pbank = {}, {}, {}, {}
+        raw, xi, cu, cv, tb, tcod, pcod, banks, planes, pmix, prod, tmix, tpl, xbank = ({} for _ in range(14))
+        obank = {}
         ocount = {}
 
         def load_x(m, h, g):
@@ -62,45 +63,38 @@ def tile_regmeangramdescentmerge_kernel(tc, x, u, v, c, tau_bytes, tau_scale, w0
             nc.sync.dma_start(out=b[:].rearrange("p g t f -> p g (t f)"),
                               in_=tau_bytes[m].rearrange("(g p t) f -> p g (t f)", p=P, t=PACK))
 
-        def inter(eng, m, h, g, lo=0, hi=H):
-            if lo == 0:
-                xt = pool.tile([P, H * PACK], BF16, name="xi", bufs=2, align_bytes=64)
+        def xmm(m, h, g):
+            if (m, h) not in xi:
+                xt = pool.tile([P, NG, H * PACK], BF16, name="xi", bufs=2, align_bytes=64)
                 xi[m, h] = xt
-            src = raw[m, h][:, g, :, lo:hi].rearrange("p t (c i) -> p c t i", i=4)
-            dst = xi[m, h][:, lo * PACK:hi * PACK].rearrange("p (c i t) -> p c t i", i=4, t=PACK)
-            eng(out=dst, in_=src)
+            for half in range(2):
+                bank = psum.tile([P, 2 * H], BF16, name="ob")
+                xbank[m, h, g, half] = bank
+                for w in range(2):
+                    j = 2 * half + w
+                    nc.tensor.matmul(out=bank[:, w * H:(w + 1) * H], lhsT=ident[:],
+                                     rhs=raw[m, h][:, g, :, j:H:PACK].rearrange("p t n -> p n t"),
+                                     start=True, stop=True)
 
-        def gain(m, h, g, op):
+        def xev(m, h, g):
+            for half in range(2):
+                nc.scalar.copy(out=xi[m, h][:, g, half * 2 * H:(half + 1) * 2 * H], in_=xbank[m, h, g, half][:])
+
+        def gain(m, h, op, g):
             if (m, h, op) not in prod:
                 pt = pool.tile([P, NG, H * PACK], BF16, name="prod", bufs=4, align_bytes=64)
                 prod[m, h, op] = pt
-            col = 6 * op + 2 * m + g
-            nc.vector.tensor_tensor(
-                out=prod[m, h, op][:, g].rearrange("p (b n t) -> p b n t", b=PACK, t=PACK),
-                in0=xi[m, h][:].rearrange("p (n b t) -> p b n t", b=PACK, t=PACK),
-                in1=gains[:, col].unsqueeze(1).unsqueeze(1).broadcast_to([P, PACK, P, PACK]),
-                op=ALU.mult)
-
-        def diags(eng, m):
-            for op in range(2):
-                for t in range(PACK):
-                    dt_ = pool.tile([P, P], BF16, name="dg", bufs=24)
-                    dg[m, op, t] = dt_
-                    eng.tensor_scalar(out=dt_[:], in0=ident[:], scalar1=gains[:, 6 * op + 2 * m + 1, t:t + 1], scalar2=None, op0=ALU.mult)
-
-        def pmm(m, h, op):
-            if (m, h, op) not in prod:
-                pt = pool.tile([P, NG, H * PACK], BF16, name="prod", bufs=4, align_bytes=64)
-                prod[m, h, op] = pt
-            for b in range(PACK):
-                bank = psum.tile([P, PACK, P], F32, name="ob")
-                pbank[m, h, op, b] = bank
-                for t in range(PACK):
-                    nc.tensor.matmul(out=bank[:, t], lhsT=dg[m, op, t][:], rhs=raw[m, h][:, 1, t, b:H:PACK], start=True, stop=True)
-
-        def pev(m, h, op, b):
-            nc.scalar.copy(out=prod[m, h, op][:, 1, b * H:(b + 1) * H].rearrange("p (n t) -> p n t", t=PACK),
-                           in_=pbank[m, h, op, b][:].rearrange("p t n -> p n t"))
+            col = 6 * op + 2 * m
+            if g is None:
+                nc.vector.tensor_tensor(
+                    out=prod[m, h, op][:].rearrange("p g (d t) -> p g d t", t=PACK),
+                    in0=xi[m, h][:].rearrange("p g (d t) -> p g d t", t=PACK),
+                    in1=gains[:, col:col + NG].unsqueeze(2).broadcast_to([P, NG, H, PACK]), op=ALU.mult)
+            else:
+                nc.vector.tensor_tensor(
+                    out=prod[m, h, op][:, g].rearrange("p (d t) -> p d t", t=PACK),
+                    in0=xi[m, h][:, g].rearrange("p (d t) -> p d t", t=PACK),
+                    in1=gains[:, col + g].unsqueeze(1).broadcast_to([P, H, PACK]), op=ALU.mult)
 
         def quant_x(m, h, op):
             if op == 0:
@@ -125,6 +119,16 @@ def tile_regmeangramdescentmerge_kernel(tc, x, u, v, c, tau_bytes, tau_scale, w0
         def tint(m, g):
             tm = pool.tile([P, F * PACK], BF16, name="tm", bufs=2, align_bytes=64)
             tmix[m, g] = tm
+            if (m, g) in TP:
+                for half in range(2):
+                    bank = psum.tile([P, 2 * H], BF16, name="ob")
+                    for w in range(2):
+                        j = 2 * half + w
+                        nc.tensor.matmul(out=bank[:, w * H:(w + 1) * H], lhsT=ident[:],
+                                         rhs=tpl[m, g][:, :, j * P:(j + 1) * P].rearrange("p t n -> p n t"),
+                                         start=True, stop=True)
+                    nc.scalar.copy(out=tm[:, half * 2 * H:(half + 1) * 2 * H], in_=bank[:])
+                return
             eng = nc.vector.tensor_copy if (m, g) in TV else nc.scalar.copy
             eng(out=tm[:].rearrange("p (c i t) -> p c t i", i=4, t=PACK),
                 in_=tpl[m, g][:].rearrange("p t (c i) -> p c t i", i=4))
@@ -150,33 +154,28 @@ def tile_regmeangramdescentmerge_kernel(tc, x, u, v, c, tau_bytes, tau_scale, w0
                         rhs_scale=cu[m, gp][1][:, k],
                         start=(k == 0), stop=(k == NG - 1))
 
-        def evac(un, t):
+        def front(un):
             m, gp, g = un
-            if un not in planes:
-                pl = pool.tile([P, PACK, H], BF16, name="pl", bufs=2)
-                planes[un] = pl
-            parts = [(0, H)] if gp != g else [(a, b) for (a, b) in ((0, t * P), ((t + 1) * P, H)) if b > a]
-            for a, b in parts:
-                nc.scalar.activation(out=planes[un][:, t, a:b], in_=banks[un][t][:, a:b], func=COPY,
-                                     scale=cs[:, 2 * m + g, t:t + 1])
-
-        def diag(un, t):
-            m, gp, g = un
-            if t == 0:
-                pl = pool.tile([P, PACK, H], BF16, name="pl", bufs=2)
-                planes[un] = pl
-            if gp == g:
-                win = slice(t * P, (t + 1) * P)
-                nc.vector.scalar_tensor_tensor(
-                    out=planes[un][:, t, win], in0=banks[un][t][:, win], scalar=cs[:, 2 * m + g, t:t + 1],
-                    in1=boost[:], op0=ALU.mult, op1=ALU.mult)
+            pl = pool.tile([P, PACK, H], BF16, name="pl", bufs=2)
+            planes[un] = pl
+            for t in range(PACK):
+                parts = [(0, H)]
+                if gp == g:
+                    parts = [(a, b) for (a, b) in ((0, t * P), ((t + 1) * P, H)) if b > a]
+                    win = slice(t * P, (t + 1) * P)
+                    nc.vector.scalar_tensor_tensor(
+                        out=pl[:, t, win], in0=banks[un][t][:, win], scalar=cs[:, 2 * m + g, t:t + 1],
+                        in1=boost[:], op0=ALU.mult, op1=ALU.mult)
+                for a, b in parts:
+                    nc.scalar.activation(out=pl[:, t, a:b], in_=banks[un][t][:, a:b], func=COPY,
+                                         scale=cs[:, 2 * m + g, t:t + 1])
 
         def pint(un):
             pm = pool.tile([P, H * PACK], BF16, name="pm", bufs=2, align_bytes=64)
             pmix[un] = pm
             eng = nc.scalar.copy if UNITS.index(un) in PS else nc.vector.tensor_copy
             eng(out=pm[:].rearrange("p (c i t) -> p c t i", i=4, t=PACK),
-                                  in_=planes[un][:].rearrange("p t (c i) -> p c t i", i=4))
+                in_=planes[un][:].rearrange("p t (c i) -> p c t i", i=4))
 
         def quant_p(un):
             cod = pool.tile([P, H], U32, name="pc", bufs=12, align_bytes=64)
@@ -202,8 +201,8 @@ def tile_regmeangramdescentmerge_kernel(tc, x, u, v, c, tau_bytes, tau_scale, w0
                 ocount[gp, b] = n + 1
 
         def apply_all(half, last):
-            for un in UNITS:
-                if un[1] == half and (UNITS.index(un) <= UNITS.index(last)):
+            for un in UNITS[:last + 1]:
+                if un[1] == half:
                     apply(un)
 
         def finish(gp, b):
@@ -212,10 +211,9 @@ def tile_regmeangramdescentmerge_kernel(tc, x, u, v, c, tau_bytes, tau_scale, w0
                                            op0=ALU.mult, op1=ALU.add)
             nc.sync.dma_start(out=out.rearrange("(g p b) f -> g b p f", g=2, b=PACK)[gp, b], in_=o[:])
 
-
-        nc.vector.memset(rows[:], 0.0)
+        nc.gpsimd.memset(rows[:], 0.0)
         for i, src in enumerate((u, v, c)):
-            nc.scalar.dma_start(out=rows[6 * i:6 * i + 6, :], in_=src.rearrange("m (g k) -> (m g) k", g=NG))
+            nc.sync.dma_start(out=rows[6 * i:6 * i + 6, :], in_=src.rearrange("m (g k) -> (m g) k", g=NG))
         load_x(0, 0, 0)
         load_x(0, 0, 1)
         nc.scalar.dma_start(out=ts[:], in_=tau_scale.rearrange("o (g p t) z -> p (o g) (t z)", p=P, t=PACK))
@@ -237,35 +235,30 @@ def tile_regmeangramdescentmerge_kernel(tc, x, u, v, c, tau_bytes, tau_scale, w0
         for t in range(PACK):
             nc.tensor.transpose(tg[:, t], rows[:, t:KP:PACK], ident[:])
         nc.vector.tensor_copy(out=gains[:], in_=tg[:, :, 0:12].rearrange("p t r -> p r t"))
-        diags(nc.vector, 0)
+
+        xt = pool.tile([P, NG, H * PACK], BF16, name="xi", bufs=2, align_bytes=64)
+        xi[0, 0] = xt
+        for eng, half in ((nc.vector.tensor_copy, 0), (nc.scalar.copy, 1)):
+            eng(out=xt[:, 0, half * 2 * H:(half + 1) * 2 * H].rearrange("p (j n t) -> p j n t", j=2, t=PACK),
+                in_=raw[0, 0][:, 0].rearrange("p t (n j) -> p j n t", j=PACK)[:, 2 * half:2 * half + 2])
+        xmm(0, 0, 1)
+        xev(0, 0, 1)
+        for g in range(NG):
+            gain(0, 0, 0, g)
+            gain(0, 0, 1, g)
         nc.vector.tensor_scalar(out=cs[:], in0=tg[:, :, 12:18].rearrange("p t r -> p r t"), scalar1=SHRINK / T,
                                 scalar2=None, op0=ALU.mult)
         nc.vector.tensor_scalar(out=boost[:], in0=ident[:], scalar1=0.25, scalar2=1.0, op0=ALU.mult, op1=ALU.add)
-        diags(nc.vector, 1)
-        diags(nc.vector, 2)
-
-        pmm(0, 0, 0)
-        inter(nc.vector.tensor_copy, 0, 0, 0)
-        for b in range(PACK):
-            pev(0, 0, 0, b)
-        gain(0, 0, 0, 0)
-        pmm(0, 0, 1)
-        for b in range(PACK):
-            pev(0, 0, 1, b)
-        gain(0, 0, 0, 1)
-        inter(nc.vector.tensor_copy, 0, 1, 0)
+        xmm(0, 1, 0)
+        xev(0, 1, 0)
+        xmm(0, 1, 1)
+        xev(0, 1, 1)
         quant_x(0, 0, 0)
-        gain(0, 1, 0, 0)
         quant_x(0, 0, 1)
-        pmm(0, 1, 0)
-        for b in range(PACK):
-            pev(0, 1, 0, b)
         gram(UNITS[0])
-        pmm(0, 1, 1)
-        for b in range(PACK):
-            pev(0, 1, 1, b)
 
-        plan = {1: UNITS[0:1], 2: UNITS[1:3], 3: UNITS[3:5], 4: UNITS[5:7], 5: UNITS[7:9]}
+        plan = {1: (), 2: (0, 1), 3: (2, 3), 4: (4, 5), 5: (6, 7)}
+        tau_at = {1: (0,), 2: (1,), 3: (2,), 4: (3,), 5: (4, 5)}
         for k in range(1, 6):
             m, h = CHUNKS[k]
             todo = plan[k]
@@ -275,72 +268,48 @@ def tile_regmeangramdescentmerge_kernel(tc, x, u, v, c, tau_bytes, tau_scale, w0
             if k == 2:
                 load_x(2, 1, 0)
                 load_x(2, 1, 1)
-            a = todo[0]
-            b = todo[1] if len(todo) > 1 else None
-            jt = ((k - 1) // 2, (k - 1) % 2)
-            gain(m, h, 0, 1)
-            for t in range(PACK):
-                diag(a, t)
-                evac(a, t)
+            gain(m, h, 0, None)
             if nxt:
-                pmm(*nxt, 0)
-            if b:
-                gram(b)
+                xmm(*nxt, 0)
+                xev(*nxt, 0)
+            gain(m, h, 1, None)
             quant_x(m, h, 0)
-            if nxt:
-                for w in range(PACK):
-                    pev(*nxt, 0, w)
-            pint(a)
+            if todo:
+                front(UNITS[todo[0]])
+                gram(UNITS[todo[0] + 1])
             quant_x(m, h, 1)
-            quant_p(a)
+            if todo:
+                pint(UNITS[todo[0]])
+                quant_p(UNITS[todo[0]])
             if nxt:
-                pmm(*nxt, 1)
-                inter(nc.vector.tensor_copy, *nxt, 0)
-            if b:
-                for t in range(PACK):
-                    diag(b, t)
-                    evac(b, t)
-            if nxt:
-                gain(*nxt, 0, 0)
-            gram(plan[k + 1][0] if k < 5 else UNITS[9])
-            widen(*jt)
-            if nxt:
-                for w in range(PACK):
-                    pev(*nxt, 1, w)
-            if b:
-                pint(b)
-                if k == 5:
-                    apply_all(0, UNITS[7])
-            tint(*jt)
-            if b:
-                quant_p(b)
-            quant_tau(*jt)
-            if k == 5:
-                widen(2, 1)
+                xmm(*nxt, 1)
+                xev(*nxt, 1)
+            if len(todo) > 1:
+                front(UNITS[todo[1]])
+                gram(UNITS[todo[1] + 1])
+                pint(UNITS[todo[1]])
+                quant_p(UNITS[todo[1]])
+            for j in tau_at[k]:
+                widen(j // 2, j % 2)
+                tint(j // 2, j % 2)
+                quant_tau(j // 2, j % 2)
 
-        u9, u10, u11 = UNITS[9:12]
-        for t in range(PACK):
-            evac(u9, t)
-        gram(u10)
-        apply(UNITS[8])
-        tint(2, 1)
-        pint(u9)
-        quant_tau(2, 1)
-        for t in range(PACK):
-            diag(u10, t)
-            evac(u10, t)
-        quant_p(u9)
-        gram(u11)
-        apply(u9)
-        pint(u10)
-        for t in range(PACK):
-            evac(u11, t)
-        for b in range(PACK):
-            finish(0, b)
-        quant_p(u10)
-        pint(u11)
-        quant_p(u11)
-        apply_all(1, u10)
-        apply(u11)
+        first = plan[5][-1] + 1
+        apply_all(0, first - 1)
+        for i in range(first, len(UNITS)):
+            un = UNITS[i]
+            front(un)
+            if i + 1 < len(UNITS):
+                gram(UNITS[i + 1])
+            pint(un)
+            quant_p(un)
+            if un[1] == 0:
+                apply(un)
+            if i == 9:
+                for b in range(PACK):
+                    finish(0, b)
+            if i == 10:
+                apply_all(1, i)
+        apply(UNITS[11])
         for b in range(PACK):
             finish(1, b)

@@ -13,303 +13,355 @@ PACK = 4
 KP = P * PACK
 NG = T // KP
 H = 512
+NW = H // P
+HALVES = D // H
+RUN = 4
+U_GAIN, V_GAIN = 0, 1
 
 F32 = mybir.dt.float32
 BF16 = mybir.dt.bfloat16
 U32 = mybir.dt.uint32
 U8 = mybir.dt.uint8
-E4 = mybir.dt.float8_e4m3fn
-X4 = mybir.dt.float8_e4m3fn_x4
+E4M3 = mybir.dt.float8_e4m3fn
+E4M3X4 = mybir.dt.float8_e4m3fn_x4
 ALU = mybir.AluOpType
 COPY = mybir.ActivationFunctionType.Copy
 
-TV = ()
-TP = ()
-PS = ()
-UNITS = [(m, gp, g) for m in range(M - 1) for (gp, g) in ((0, 0), (0, 1), (1, 0), (1, 1))] + [
+CHUNKS = [(m, h) for m in range(M) for h in range(HALVES)]
+GAIN_ORDER = ((U_GAIN, V_GAIN), (V_GAIN, U_GAIN))
+
+UNITS = [(m, h, g) for m in range(M - 1) for h in range(HALVES) for g in range(NG)] + [
     (M - 1, 0, 0), (M - 1, 0, 1), (M - 1, 1, 1), (M - 1, 1, 0)]
-CHUNKS = [(m, h) for m in range(M) for h in range(2)]
+UNITS_BESIDE = {1: (0,), 2: (1, 2), 3: (3, 4), 4: (5, 6), 5: (7, 8)}
+FIRST_TAIL_UNIT = 9
+LAST_UNIT = len(UNITS) - 1
+TAU_MIX_ON_SCALAR = ((0, 0),)
+P_MIX_ON_SCALAR = (9, 10)
 
 
 def tile_regmeangramdescentmerge_kernel(tc, x, u, v, c, tau_bytes, tau_scale, w0, out):
     nc = tc.nc
     with ExitStack() as ctx:
-        pool = ctx.enter_context(tc.tile_pool(name="sb", bufs=1))
-        psum = ctx.enter_context(tc.psum_pool(name="ps", bufs=4))
+        pool = ctx.enter_context(tc.tile_pool(name="sbuf", bufs=1))
+        psum = ctx.enter_context(tc.psum_pool(name="psum", bufs=4))
 
         ident = pool.tile([P, P], BF16, name="ident")
         boost = pool.tile([P, P], F32, name="boost")
-        rows = pool.tile([P, KP], BF16, name="rows")
-        gains = pool.tile([P, 12, PACK], BF16, name="gains")
-        cs = pool.tile([P, 6, PACK], F32, name="cs")
-        ts = pool.tile([P, NG, PACK], F32, name="ts")
-        w0_sb = pool.tile([P, 2, PACK, F], BF16, name="w0_sb")
+        u_first = pool.tile([P, NG, PACK], BF16, name="u_first")
+        v_first = pool.tile([P, NG, PACK], BF16, name="v_first")
+        u_rest = pool.tile([P, (M - 1) * NG, PACK], BF16, name="u_rest")
+        v_rest = pool.tile([P, (M - 1) * NG, PACK], BF16, name="v_rest")
+        c_gain = pool.tile([P, M * NG, PACK], BF16, name="c_gain")
+        c_scaled = pool.tile([P, M * NG, PACK], F32, name="c_scaled")
+        tau_scales = pool.tile([P, NG, PACK], F32, name="tau_scales")
+        w0_sb = pool.tile([P, HALVES, NW, F], BF16, name="w0_sb")
 
-        raw, xi, cu, cv, tb, tcod, pcod, banks, planes, pmix, prod, tmix, tpl, xbank = ({} for _ in range(14))
-        obank = {}
-        ocount = {}
+        raw, mixed, products, gain_banks, diagonal = {}, {}, {}, {}, {}
+        xu_codes, xv_codes, gram_banks, p_rows, p_mixed, p_codes = {}, {}, {}, {}, {}, {}
+        tau_raw, tau_rows, tau_mixed, tau_codes = {}, {}, {}, {}
+        out_banks, out_passes = {}, {}
+
 
         def load_x(m, h, g):
             if g == 0:
-                r = pool.tile([P, NG, PACK, H], BF16, name="raw", bufs=5)
-                raw[m, h] = r
+                tile = pool.tile([P, NG, PACK, H], BF16, name="raw", bufs=5)
+                raw[m, h] = tile
             nc.sync.dma_start(
                 out=raw[m, h][:, g],
                 in_=x[m, g * KP:(g + 1) * KP, h * H:(h + 1) * H].rearrange("(p t) d -> p t d", t=PACK))
 
         def load_tau(m):
-            b = pool.tile([P, NG, PACK, F], U8, name="tb", bufs=2)
-            tb[m] = b
-            nc.sync.dma_start(out=b[:].rearrange("p g t f -> p g (t f)"),
+            tile = pool.tile([P, NG, PACK, F], U8, name="tau_raw", bufs=2)
+            tau_raw[m] = tile
+            nc.sync.dma_start(out=tile[:].rearrange("p g t f -> p g (t f)"),
                               in_=tau_bytes[m].rearrange("(g p t) f -> p g (t f)", p=P, t=PACK))
 
-        def xmm(m, h, g):
-            if (m, h) not in xi:
-                xt = pool.tile([P, NG, H * PACK], BF16, name="xi", bufs=2, align_bytes=64)
-                xi[m, h] = xt
-            for half in range(2):
-                bank = psum.tile([P, 2 * H], BF16, name="ob")
-                xbank[m, h, g, half] = bank
-                for w in range(2):
-                    j = 2 * half + w
-                    nc.tensor.matmul(out=bank[:, w * H:(w + 1) * H], lhsT=ident[:],
-                                     rhs=raw[m, h][:, g, :, j:H:PACK].rearrange("p t n -> p n t"),
-                                     start=True, stop=True)
+        def load_gains(m0, m1, u_tile, v_tile):
+            for tile, source in ((u_tile, u), (v_tile, v)):
+                nc.sync.dma_start(out=tile[:], in_=source[m0:m1].rearrange("m (g p t) -> p (m g) t", p=P, t=PACK))
 
-        def xev(m, h, g):
-            for half in range(2):
-                nc.scalar.copy(out=xi[m, h][:, g, half * 2 * H:(half + 1) * 2 * H], in_=xbank[m, h, g, half][:])
+        def token_gain(which, m, g):
+            if m == 0:
+                return (u_first, v_first)[which][:, g]
+            return (u_rest, v_rest)[which][:, (m - 1) * NG + g]
 
-        def gain(m, h, op, g):
-            if (m, h, op) not in prod:
-                pt = pool.tile([P, NG, H * PACK], BF16, name="prod", bufs=4, align_bytes=64)
-                prod[m, h, op] = pt
-            col = 6 * op + 2 * m
-            if g is None:
+
+        def product_tile(m, h, which):
+            if (m, h, which) not in products:
+                tile = pool.tile([P, NG, H * PACK], BF16, name="products", bufs=4, align_bytes=64)
+                products[m, h, which] = tile
+            return products[m, h, which]
+
+        def mix_x(copy, m, h, lo=0, hi=H):
+            if lo == 0:
+                tile = pool.tile([P, H * PACK], BF16, name="mixed", bufs=2, align_bytes=64)
+                mixed[m, h] = tile
+            copy(out=mixed[m, h][:, lo * PACK:hi * PACK].rearrange("p (c i t) -> p c t i", i=RUN, t=PACK),
+                 in_=raw[m, h][:, 0, :, lo:hi].rearrange("p t (c i) -> p c t i", i=RUN))
+
+        def gain_on_vector(m, h, which):
+            target = product_tile(m, h, which)
+            gain = token_gain(which, m, 0)
+            if which == U_GAIN:
                 nc.vector.tensor_tensor(
-                    out=prod[m, h, op][:].rearrange("p g (d t) -> p g d t", t=PACK),
-                    in0=xi[m, h][:].rearrange("p g (d t) -> p g d t", t=PACK),
-                    in1=gains[:, col:col + NG].unsqueeze(2).broadcast_to([P, NG, H, PACK]), op=ALU.mult)
+                    out=target[:, 0].rearrange("p (d t) -> p d t", t=PACK),
+                    in0=mixed[m, h][:].rearrange("p (d t) -> p d t", t=PACK),
+                    in1=gain.unsqueeze(1).broadcast_to([P, H, PACK]), op=ALU.mult)
             else:
                 nc.vector.tensor_tensor(
-                    out=prod[m, h, op][:, g].rearrange("p (d t) -> p d t", t=PACK),
-                    in0=xi[m, h][:, g].rearrange("p (d t) -> p d t", t=PACK),
-                    in1=gains[:, col + g].unsqueeze(1).broadcast_to([P, H, PACK]), op=ALU.mult)
+                    out=target[:, 0].rearrange("p (j n t) -> p j n t", j=NW, t=PACK),
+                    in0=mixed[m, h][:].rearrange("p (n j t) -> p j n t", j=NW, t=PACK),
+                    in1=gain.unsqueeze(1).unsqueeze(1).broadcast_to([P, NW, P, PACK]), op=ALU.mult)
 
-        def quant_x(m, h, op):
-            if op == 0:
-                cod = pool.tile([P, NG, H], U32, name="cu", bufs=4, align_bytes=64)
-                sca = pool.tile([P, NG, H], U8, name="cus", bufs=4, align_bytes=64)
-                cu[m, h] = (cod, sca)
-            else:
-                cod = pool.tile([P, NG, H], U32, name="cv", bufs=4, align_bytes=64)
-                sca = pool.tile([P, NG, H], U8, name="cvs", bufs=4, align_bytes=64)
-                cv[m, h] = (cod, sca)
+        def make_diagonals(m):
+            for which in (U_GAIN, V_GAIN):
+                for t in range(PACK):
+                    tile = pool.tile([P, P], BF16, name="diagonal", bufs=M * 2 * PACK)
+                    diagonal[m, which, t] = tile
+                    nc.vector.tensor_scalar(out=tile[:], in0=ident[:], scalar1=token_gain(which, m, 1)[:, t:t + 1],
+                                            scalar2=None, op0=ALU.mult)
+
+        def gain_on_tensor(m, h, which):
+            product_tile(m, h, which)
+            for part in range(2):
+                bank = psum.tile([P, PACK, H // 2], BF16, name="gain_bank", bufs=2)
+                gain_banks[m, h, which, part] = bank
+                for t in range(PACK):
+                    nc.tensor.matmul(out=bank[:, t], lhsT=diagonal[m, which, t][:],
+                                     rhs=raw[m, h][:, 1, t, part * H // 2:(part + 1) * H // 2], start=True, stop=True)
+
+        def copy_gain_banks(m, h, which):
+            target = products[m, h, which][:, 1]
+            for part in range(2):
+                bank = gain_banks[m, h, which, part]
+                if which == U_GAIN:
+                    nc.scalar.copy(
+                        out=target[:, part * 2 * H:(part + 1) * 2 * H].rearrange("p (d t) -> p d t", t=PACK),
+                        in_=bank[:].rearrange("p t d -> p d t"))
+                else:
+                    nc.scalar.copy(
+                        out=target.rearrange("p (j part n t) -> p part j n t", j=NW, part=2, t=PACK)[:, part],
+                        in_=bank[:].rearrange("p t (n j) -> p j n t", j=NW))
+
+        def quantise_x(m, h, which):
+            name = ("xu", "xv")[which]
+            codes = pool.tile([P, NG, H], U32, name=name + "_codes", bufs=4, align_bytes=64)
+            scales = pool.tile([P, NG, H], U8, name=name + "_scales", bufs=4, align_bytes=64)
+            (xu_codes, xv_codes)[which][m, h] = (codes, scales)
             nc.vector.quantize_mx(
-                out=cod[:].rearrange("p g d -> p (g d)").bitcast(X4),
-                scales=sca[:].rearrange("p g d -> p (g d)"),
-                in_=prod[m, h, op][:].rearrange("p g d -> p (g d)"))
+                out=codes[:].rearrange("p g d -> p (g d)").bitcast(E4M3X4),
+                scales=scales[:].rearrange("p g d -> p (g d)"),
+                in_=products[m, h, which][:].rearrange("p g d -> p (g d)"))
 
-        def widen(m, g):
-            tp = pool.tile([P, PACK, F], BF16, name="tp", bufs=2)
+
+        def widen_tau(m, g):
+            tile = pool.tile([P, PACK, F], BF16, name="tau_rows", bufs=2)
+            tau_rows[m, g] = tile
             for t in range(PACK):
-                nc.scalar.activation(out=tp[:, t], in_=tb[m][:, g, t].bitcast(E4), func=COPY, scale=ts[:, g, t:t + 1])
-            tpl[m, g] = tp
+                nc.scalar.activation(out=tile[:, t], in_=tau_raw[m][:, g, t].bitcast(E4M3), func=COPY,
+                                     scale=tau_scales[:, g, t:t + 1])
 
-        def tint(m, g):
-            tm = pool.tile([P, F * PACK], BF16, name="tm", bufs=2, align_bytes=64)
-            tmix[m, g] = tm
-            if (m, g) in TP:
-                for half in range(2):
-                    bank = psum.tile([P, 2 * H], BF16, name="ob")
-                    for w in range(2):
-                        j = 2 * half + w
-                        nc.tensor.matmul(out=bank[:, w * H:(w + 1) * H], lhsT=ident[:],
-                                         rhs=tpl[m, g][:, :, j * P:(j + 1) * P].rearrange("p t n -> p n t"),
-                                         start=True, stop=True)
-                    nc.scalar.copy(out=tm[:, half * 2 * H:(half + 1) * 2 * H], in_=bank[:])
-                return
-            eng = nc.vector.tensor_copy if (m, g) in TV else nc.scalar.copy
-            eng(out=tm[:].rearrange("p (c i t) -> p c t i", i=4, t=PACK),
-                in_=tpl[m, g][:].rearrange("p t (c i) -> p c t i", i=4))
+        def mix_tau(m, g):
+            tile = pool.tile([P, F * PACK], BF16, name="tau_mixed", bufs=2, align_bytes=64)
+            tau_mixed[m, g] = tile
+            copy = nc.scalar.copy if (m, g) in TAU_MIX_ON_SCALAR else nc.vector.tensor_copy
+            copy(out=tile[:].rearrange("p (c i t) -> p c t i", i=RUN, t=PACK),
+                 in_=tau_rows[m, g][:].rearrange("p t (c i) -> p c t i", i=RUN))
 
-        def quant_tau(m, g):
-            cod = pool.tile([P, F], U32, name="tc", bufs=6, align_bytes=64)
-            sca = pool.tile([P, F], U8, name="tcs", bufs=6, align_bytes=64)
-            tcod[m, g] = (cod, sca)
-            nc.vector.quantize_mx(out=cod[:].bitcast(X4), scales=sca[:], in_=tmix[m, g][:])
+        def quantise_tau(m, g):
+            codes = pool.tile([P, F], U32, name="tau_codes", bufs=M * NG, align_bytes=64)
+            scales = pool.tile([P, F], U8, name="tau_code_scales", bufs=M * NG, align_bytes=64)
+            tau_codes[m, g] = (codes, scales)
+            nc.vector.quantize_mx(out=codes[:].bitcast(E4M3X4), scales=scales[:], in_=tau_mixed[m, g][:])
 
-        def gram(un):
-            m, gp, g = un
-            banks[un] = []
+
+        def gram(unit):
+            m, h, g = unit
+            gram_banks[unit] = []
             for t in range(PACK):
-                bank = psum.tile([P, H], F32, name="gr")
-                banks[un].append(bank)
+                bank = psum.tile([P, H], F32, name="gram_bank")
+                gram_banks[unit].append(bank)
                 for k in range(NG):
                     nc.tensor.matmul_mx(
                         out=bank[:],
-                        lhsT=cv[m, g][0][:, k, t * P:(t + 1) * P].bitcast(X4),
-                        lhsT_scale=cv[m, g][1][:, k, t * P:(t + 1) * P],
-                        rhs=cu[m, gp][0][:, k].bitcast(X4),
-                        rhs_scale=cu[m, gp][1][:, k],
+                        lhsT=xv_codes[m, g][0][:, k, t * P:(t + 1) * P].bitcast(E4M3X4),
+                        lhsT_scale=xv_codes[m, g][1][:, k, t * P:(t + 1) * P],
+                        rhs=xu_codes[m, h][0][:, k].bitcast(E4M3X4),
+                        rhs_scale=xu_codes[m, h][1][:, k],
                         start=(k == 0), stop=(k == NG - 1))
 
-        def front(un):
-            m, gp, g = un
-            pl = pool.tile([P, PACK, H], BF16, name="pl", bufs=2)
-            planes[un] = pl
+        def scale_gram(unit):
+            m, h, g = unit
+            rows = pool.tile([P, PACK, H], BF16, name="p_rows", bufs=2)
+            p_rows[unit] = rows
             for t in range(PACK):
-                parts = [(0, H)]
-                if gp == g:
-                    parts = [(a, b) for (a, b) in ((0, t * P), ((t + 1) * P, H)) if b > a]
-                    win = slice(t * P, (t + 1) * P)
+                windows = gram_banks[unit][t][:].rearrange("p (n j) -> p j n", j=NW)
+                factor = c_scaled[:, NG * m + g, t:t + 1]
+                spans = [(0, NW)]
+                if h == g:
+                    spans = [(lo, hi) for (lo, hi) in ((0, t), (t + 1, NW)) if hi > lo]
                     nc.vector.scalar_tensor_tensor(
-                        out=pl[:, t, win], in0=banks[un][t][:, win], scalar=cs[:, 2 * m + g, t:t + 1],
-                        in1=boost[:], op0=ALU.mult, op1=ALU.mult)
-                for a, b in parts:
-                    nc.scalar.activation(out=pl[:, t, a:b], in_=banks[un][t][:, a:b], func=COPY,
-                                         scale=cs[:, 2 * m + g, t:t + 1])
+                        out=rows[:, t, t * P:(t + 1) * P], in0=windows[:, t], scalar=factor, in1=boost[:],
+                        op0=ALU.mult, op1=ALU.mult)
+                for lo, hi in spans:
+                    nc.scalar.activation(out=rows[:, t, lo * P:hi * P].rearrange("p (j n) -> p j n", n=P),
+                                         in_=windows[:, lo:hi], func=COPY, scale=factor)
 
-        def pint(un):
-            pm = pool.tile([P, H * PACK], BF16, name="pm", bufs=2, align_bytes=64)
-            pmix[un] = pm
-            eng = nc.scalar.copy if UNITS.index(un) in PS else nc.vector.tensor_copy
-            eng(out=pm[:].rearrange("p (c i t) -> p c t i", i=4, t=PACK),
-                in_=planes[un][:].rearrange("p t (c i) -> p c t i", i=4))
+        def mix_p(unit):
+            tile = pool.tile([P, H * PACK], BF16, name="p_mixed", bufs=2, align_bytes=64)
+            p_mixed[unit] = tile
+            copy = nc.scalar.copy if UNITS.index(unit) in P_MIX_ON_SCALAR else nc.vector.tensor_copy
+            copy(out=tile[:].rearrange("p (c i t) -> p c t i", i=RUN, t=PACK),
+                 in_=p_rows[unit][:].rearrange("p t (c i) -> p c t i", i=RUN))
 
-        def quant_p(un):
-            cod = pool.tile([P, H], U32, name="pc", bufs=12, align_bytes=64)
-            sca = pool.tile([P, H], U8, name="pcs", bufs=12, align_bytes=64)
-            pcod[un] = (cod, sca)
-            nc.vector.quantize_mx(out=cod[:].bitcast(X4), scales=sca[:], in_=pmix[un][:])
+        def quantise_p(unit):
+            codes = pool.tile([P, H], U32, name="p_codes", bufs=len(UNITS), align_bytes=64)
+            scales = pool.tile([P, H], U8, name="p_scales", bufs=len(UNITS), align_bytes=64)
+            p_codes[unit] = (codes, scales)
+            nc.vector.quantize_mx(out=codes[:].bitcast(E4M3X4), scales=scales[:], in_=p_mixed[unit][:])
 
-        def apply(un):
-            m, gp, g = un
-            for b in range(PACK):
-                if (gp, b) not in obank:
-                    ob = psum.tile([P, F], F32, name="ob")
-                    obank[gp, b] = ob
-                    ocount[gp, b] = 0
-                n = ocount[gp, b]
+
+        def apply(unit, pair):
+            m, h, g = unit
+            for j in (2 * pair, 2 * pair + 1):
+                if (h, j) not in out_banks:
+                    bank = psum.tile([P, F], F32, name="out_bank", tag=("out_bank", "gain_bank")[pair], bufs=2)
+                    out_banks[h, j] = bank
+                    out_passes[h, j] = 0
+                done = out_passes[h, j]
                 nc.tensor.matmul_mx(
-                    out=obank[gp, b][:],
-                    lhsT=pcod[un][0][:, b * P:(b + 1) * P].bitcast(X4),
-                    lhsT_scale=pcod[un][1][:, b * P:(b + 1) * P],
-                    rhs=tcod[m, g][0][:].bitcast(X4),
-                    rhs_scale=tcod[m, g][1][:],
-                    start=(n == 0), stop=(n == 2 * M - 1))
-                ocount[gp, b] = n + 1
+                    out=out_banks[h, j][:],
+                    lhsT=p_codes[unit][0][:, j * P:(j + 1) * P].bitcast(E4M3X4),
+                    lhsT_scale=p_codes[unit][1][:, j * P:(j + 1) * P],
+                    rhs=tau_codes[m, g][0][:].bitcast(E4M3X4),
+                    rhs_scale=tau_codes[m, g][1][:],
+                    start=(done == 0), stop=(done == M * NG - 1))
+                out_passes[h, j] = done + 1
 
-        def apply_all(half, last):
-            for un in UNITS[:last + 1]:
-                if un[1] == half:
-                    apply(un)
-
-        def finish(gp, b):
-            o = pool.tile([P, F], F32, name="o", bufs=4)
-            nc.vector.scalar_tensor_tensor(out=o[:], in0=obank[gp, b][:], scalar=STEP, in1=w0_sb[:, gp, b],
+        def finish(h, j):
+            result = pool.tile([P, F], F32, name="result", bufs=4)
+            nc.vector.scalar_tensor_tensor(out=result[:], in0=out_banks[h, j][:], scalar=STEP, in1=w0_sb[:, h, j],
                                            op0=ALU.mult, op1=ALU.add)
-            nc.sync.dma_start(out=out.rearrange("(g p b) f -> g b p f", g=2, b=PACK)[gp, b], in_=o[:])
+            nc.sync.dma_start(out=out.rearrange("(h p j) f -> h j p f", h=HALVES, j=NW)[h, j], in_=result[:])
 
-        nc.gpsimd.memset(rows[:], 0.0)
-        for i, src in enumerate((u, v, c)):
-            nc.sync.dma_start(out=rows[6 * i:6 * i + 6, :], in_=src.rearrange("m (g k) -> (m g) k", g=NG))
-        load_x(0, 0, 0)
-        load_x(0, 0, 1)
-        nc.scalar.dma_start(out=ts[:], in_=tau_scale.rearrange("o (g p t) z -> p (o g) (t z)", p=P, t=PACK))
-        load_x(0, 1, 0)
-        load_x(0, 1, 1)
-        load_tau(0)
-        load_x(1, 0, 0)
-        load_x(1, 0, 1)
-        load_x(1, 1, 0)
-        load_x(1, 1, 1)
-        load_tau(1)
-        load_x(2, 0, 0)
-        load_x(2, 0, 1)
-        nc.sync.dma_start(out=w0_sb[:].rearrange("p g b f -> p g (b f)"),
-                          in_=w0.rearrange("(g p b) f -> p g (b f)", g=2, b=PACK))
+
         make_identity(nc, ident[:])
+        with tc.manual_schedule():
+            load_x(0, 0, 0)
+            load_gains(0, 1, u_first, v_first)
+            load_x(0, 0, 1)
+            load_x(0, 1, 0)
+            load_x(0, 1, 1)
+            nc.sync.dma_start(out=c_gain[:], in_=c.rearrange("m (g p t) -> p (m g) t", p=P, t=PACK))
+            nc.sync.dma_start(out=tau_scales[:],
+                              in_=tau_scale.rearrange("o (g p t) z -> p (o g) (t z)", p=P, t=PACK))
+            load_tau(0)
+            load_gains(1, M, u_rest, v_rest)
+            for h in range(HALVES):
+                for g in range(NG):
+                    load_x(1, h, g)
+            load_tau(1)
+            load_x(2, 0, 0)
+            load_x(2, 0, 1)
+            nc.sync.dma_start(out=w0_sb[:].rearrange("p h j f -> p h (j f)"),
+                              in_=w0.rearrange("(h p j) f -> p h (j f)", h=HALVES, j=NW))
 
-        tg = psum.tile([P, PACK, P], BF16, name="gr")
-        for t in range(PACK):
-            nc.tensor.transpose(tg[:, t], rows[:, t:KP:PACK], ident[:])
-        nc.vector.tensor_copy(out=gains[:], in_=tg[:, :, 0:12].rearrange("p t r -> p r t"))
+            mix_x(nc.vector.tensor_copy, 0, 0, 0, H // 2)
+            mix_x(nc.scalar.copy, 0, 0, H // 2, H)
+            make_diagonals(0)
+            for which in GAIN_ORDER[0]:
+                gain_on_tensor(0, 0, which)
+                copy_gain_banks(0, 0, which)
+                gain_on_vector(0, 0, which)
+            mix_x(nc.vector.tensor_copy, 0, 1)
+            quantise_x(0, 0, U_GAIN)
 
-        xt = pool.tile([P, NG, H * PACK], BF16, name="xi", bufs=2, align_bytes=64)
-        xi[0, 0] = xt
-        for eng, half in ((nc.vector.tensor_copy, 0), (nc.scalar.copy, 1)):
-            eng(out=xt[:, 0, half * 2 * H:(half + 1) * 2 * H].rearrange("p (j n t) -> p j n t", j=2, t=PACK),
-                in_=raw[0, 0][:, 0].rearrange("p t (n j) -> p j n t", j=PACK)[:, 2 * half:2 * half + 2])
-        xmm(0, 0, 1)
-        xev(0, 0, 1)
-        for g in range(NG):
-            gain(0, 0, 0, g)
-            gain(0, 0, 1, g)
-        nc.vector.tensor_scalar(out=cs[:], in0=tg[:, :, 12:18].rearrange("p t r -> p r t"), scalar1=SHRINK / T,
-                                scalar2=None, op0=ALU.mult)
+
+        first, second = GAIN_ORDER[1]
+        gain_on_vector(0, 1, first)
+        quantise_x(0, 0, V_GAIN)
+        gain_on_tensor(0, 1, first)
+        copy_gain_banks(0, 1, first)
+        nc.vector.tensor_scalar(out=c_scaled[:], in0=c_gain[:], scalar1=SHRINK / T, scalar2=None, op0=ALU.mult)
         nc.vector.tensor_scalar(out=boost[:], in0=ident[:], scalar1=0.25, scalar2=1.0, op0=ALU.mult, op1=ALU.add)
-        xmm(0, 1, 0)
-        xev(0, 1, 0)
-        xmm(0, 1, 1)
-        xev(0, 1, 1)
-        quant_x(0, 0, 0)
-        quant_x(0, 0, 1)
         gram(UNITS[0])
+        gain_on_tensor(0, 1, second)
+        copy_gain_banks(0, 1, second)
+        make_diagonals(1)
+        make_diagonals(2)
 
-        plan = {1: (), 2: (0, 1), 3: (2, 3), 4: (4, 5), 5: (6, 7)}
-        tau_at = {1: (0,), 2: (1,), 3: (2,), 4: (3,), 5: (4, 5)}
-        for k in range(1, 6):
+        for k in range(1, len(CHUNKS)):
             m, h = CHUNKS[k]
-            todo = plan[k]
-            nxt = CHUNKS[k + 1] if k < 5 else None
-            if k == 3:
-                load_tau(2)
+            first, second = GAIN_ORDER[h]
+            ahead = CHUNKS[k + 1] if k + 1 < len(CHUNKS) else None
+            units = [UNITS[i] for i in UNITS_BESIDE[k]]
+            tau_group = divmod(k - 1, NG)
             if k == 2:
                 load_x(2, 1, 0)
                 load_x(2, 1, 1)
-            gain(m, h, 0, None)
-            if nxt:
-                xmm(*nxt, 0)
-                xev(*nxt, 0)
-            gain(m, h, 1, None)
-            quant_x(m, h, 0)
-            if todo:
-                front(UNITS[todo[0]])
-                gram(UNITS[todo[0] + 1])
-            quant_x(m, h, 1)
-            if todo:
-                pint(UNITS[todo[0]])
-                quant_p(UNITS[todo[0]])
-            if nxt:
-                xmm(*nxt, 1)
-                xev(*nxt, 1)
-            if len(todo) > 1:
-                front(UNITS[todo[1]])
-                gram(UNITS[todo[1] + 1])
-                pint(UNITS[todo[1]])
-                quant_p(UNITS[todo[1]])
-            for j in tau_at[k]:
-                widen(j // 2, j % 2)
-                tint(j // 2, j % 2)
-                quant_tau(j // 2, j % 2)
+            gain_on_vector(m, h, second)
+            scale_gram(units[0])
+            if ahead:
+                ahead_first, ahead_second = GAIN_ORDER[ahead[1]]
+                gain_on_tensor(*ahead, ahead_first)
+            if len(units) > 1:
+                gram(units[1])
+            quantise_x(m, h, first)
+            if ahead:
+                copy_gain_banks(*ahead, ahead_first)
+            mix_p(units[0])
+            quantise_x(m, h, second)
+            quantise_p(units[0])
+            if ahead:
+                gain_on_tensor(*ahead, ahead_second)
+                mix_x(nc.vector.tensor_copy, *ahead)
+            if len(units) > 1:
+                scale_gram(units[1])
+            if ahead:
+                gain_on_vector(*ahead, ahead_first)
+            gram(UNITS[UNITS_BESIDE[k][-1] + 1])
+            widen_tau(*tau_group)
+            if ahead:
+                copy_gain_banks(*ahead, ahead_second)
+            if len(units) > 1:
+                mix_p(units[1])
+            mix_tau(*tau_group)
+            if k == 3:
+                load_tau(2)
+            if len(units) > 1:
+                quantise_p(units[1])
+            quantise_tau(*tau_group)
+            if k > 1:
+                for i in UNITS_BESIDE[k - 1]:
+                    if UNITS[i][1] == 0:
+                        apply(UNITS[i], 0)
+        widen_tau(M - 1, NG - 1)
+        mix_tau(M - 1, NG - 1)
+        quantise_tau(M - 1, NG - 1)
 
-        first = plan[5][-1] + 1
-        apply_all(0, first - 1)
-        for i in range(first, len(UNITS)):
-            un = UNITS[i]
-            front(un)
-            if i + 1 < len(UNITS):
+        for i in range(FIRST_TAIL_UNIT):
+            if UNITS[i][1] == 0:
+                apply(UNITS[i], 1)
+                if i in UNITS_BESIDE[len(CHUNKS) - 1]:
+                    apply(UNITS[i], 0)
+        for i in range(FIRST_TAIL_UNIT, len(UNITS)):
+            unit = UNITS[i]
+            scale_gram(unit)
+            if i < LAST_UNIT:
                 gram(UNITS[i + 1])
-            pint(un)
-            quant_p(un)
-            if un[1] == 0:
-                apply(un)
-            if i == 9:
-                for b in range(PACK):
-                    finish(0, b)
-            if i == 10:
-                apply_all(1, i)
-        apply(UNITS[11])
-        for b in range(PACK):
-            finish(1, b)
+            mix_p(unit)
+            quantise_p(unit)
+            if unit[1] == 0:
+                apply(unit, 0)
+                apply(unit, 1)
+                for j in range(NW):
+                    finish(0, j)
+            if i == LAST_UNIT - 1:
+                for earlier in UNITS[:LAST_UNIT]:
+                    if earlier[1] == 1:
+                        apply(earlier, 0)
+                        apply(earlier, 1)
+        apply(UNITS[LAST_UNIT], 0)
+        apply(UNITS[LAST_UNIT], 1)
+        for j in range(NW):
+            finish(1, j)

from contextlib import ExitStack

import concourse.mybir as mybir
from concourse.masks import make_identity

M, T, D, F = 3, 1024, 1024, 512
SHRINK, STEP = 0.8, 0.3

FLOPS = M * (2 * D * D * T + 2 * D * D * F)

P = 128
PACK = 4
KP = P * PACK
NG = T // KP
H = 512
NW = H // P
HALVES = D // H
RUN = 4
U_GAIN, V_GAIN = 0, 1

F32 = mybir.dt.float32
BF16 = mybir.dt.bfloat16
U32 = mybir.dt.uint32
U8 = mybir.dt.uint8
E4M3 = mybir.dt.float8_e4m3fn
E4M3X4 = mybir.dt.float8_e4m3fn_x4
ALU = mybir.AluOpType
COPY = mybir.ActivationFunctionType.Copy

CHUNKS = [(m, h) for m in range(M) for h in range(HALVES)]
GAIN_ORDER = ((U_GAIN, V_GAIN), (V_GAIN, U_GAIN))

UNITS = [(m, h, g) for m in range(M - 1) for h in range(HALVES) for g in range(NG)] + [
    (M - 1, 0, 0), (M - 1, 0, 1), (M - 1, 1, 1), (M - 1, 1, 0)]
UNITS_BESIDE = {1: (0,), 2: (1, 2), 3: (3, 4), 4: (5, 6), 5: (7, 8)}
FIRST_TAIL_UNIT = 9
LAST_UNIT = len(UNITS) - 1
TAU_MIX_ON_SCALAR = ((0, 0),)
P_MIX_ON_SCALAR = (9, 10)


def tile_regmeangramdescentmerge_kernel(tc, x, u, v, c, tau_bytes, tau_scale, w0, out):
    nc = tc.nc
    with ExitStack() as ctx:
        pool = ctx.enter_context(tc.tile_pool(name="sbuf", bufs=1))
        psum = ctx.enter_context(tc.psum_pool(name="psum", bufs=4))

        ident = pool.tile([P, P], BF16, name="ident")
        boost = pool.tile([P, P], F32, name="boost")
        u_first = pool.tile([P, NG, PACK], BF16, name="u_first")
        v_first = pool.tile([P, NG, PACK], BF16, name="v_first")
        u_rest = pool.tile([P, (M - 1) * NG, PACK], BF16, name="u_rest")
        v_rest = pool.tile([P, (M - 1) * NG, PACK], BF16, name="v_rest")
        c_gain = pool.tile([P, M * NG, PACK], BF16, name="c_gain")
        c_scaled = pool.tile([P, M * NG, PACK], F32, name="c_scaled")
        tau_scales = pool.tile([P, NG, PACK], F32, name="tau_scales")
        w0_sb = pool.tile([P, HALVES, NW, F], BF16, name="w0_sb")

        raw, mixed, products, gain_banks, diagonal = {}, {}, {}, {}, {}
        xu_codes, xv_codes, gram_banks, p_rows, p_mixed, p_codes = {}, {}, {}, {}, {}, {}
        tau_raw, tau_rows, tau_mixed, tau_codes = {}, {}, {}, {}
        out_banks, out_passes = {}, {}


        def load_x(m, h, g):
            if g == 0:
                tile = pool.tile([P, NG, PACK, H], BF16, name="raw", bufs=5)
                raw[m, h] = tile
            nc.sync.dma_start(
                out=raw[m, h][:, g],
                in_=x[m, g * KP:(g + 1) * KP, h * H:(h + 1) * H].rearrange("(p t) d -> p t d", t=PACK))

        def load_tau(m):
            tile = pool.tile([P, NG, PACK, F], U8, name="tau_raw", bufs=2)
            tau_raw[m] = tile
            nc.sync.dma_start(out=tile[:].rearrange("p g t f -> p g (t f)"),
                              in_=tau_bytes[m].rearrange("(g p t) f -> p g (t f)", p=P, t=PACK))

        def load_gains(m0, m1, u_tile, v_tile):
            for tile, source in ((u_tile, u), (v_tile, v)):
                nc.sync.dma_start(out=tile[:], in_=source[m0:m1].rearrange("m (g p t) -> p (m g) t", p=P, t=PACK))

        def token_gain(which, m, g):
            if m == 0:
                return (u_first, v_first)[which][:, g]
            return (u_rest, v_rest)[which][:, (m - 1) * NG + g]


        def product_tile(m, h, which):
            if (m, h, which) not in products:
                tile = pool.tile([P, NG, H * PACK], BF16, name="products", bufs=4, align_bytes=64)
                products[m, h, which] = tile
            return products[m, h, which]

        def mix_x(copy, m, h, lo=0, hi=H):
            if lo == 0:
                tile = pool.tile([P, H * PACK], BF16, name="mixed", bufs=2, align_bytes=64)
                mixed[m, h] = tile
            copy(out=mixed[m, h][:, lo * PACK:hi * PACK].rearrange("p (c i t) -> p c t i", i=RUN, t=PACK),
                 in_=raw[m, h][:, 0, :, lo:hi].rearrange("p t (c i) -> p c t i", i=RUN))

        def gain_on_vector(m, h, which):
            target = product_tile(m, h, which)
            gain = token_gain(which, m, 0)
            if which == U_GAIN:
                nc.vector.tensor_tensor(
                    out=target[:, 0].rearrange("p (d t) -> p d t", t=PACK),
                    in0=mixed[m, h][:].rearrange("p (d t) -> p d t", t=PACK),
                    in1=gain.unsqueeze(1).broadcast_to([P, H, PACK]), op=ALU.mult)
            else:
                nc.vector.tensor_tensor(
                    out=target[:, 0].rearrange("p (j n t) -> p j n t", j=NW, t=PACK),
                    in0=mixed[m, h][:].rearrange("p (n j t) -> p j n t", j=NW, t=PACK),
                    in1=gain.unsqueeze(1).unsqueeze(1).broadcast_to([P, NW, P, PACK]), op=ALU.mult)

        def make_diagonals(m):
            for which in (U_GAIN, V_GAIN):
                for t in range(PACK):
                    tile = pool.tile([P, P], BF16, name="diagonal", bufs=M * 2 * PACK)
                    diagonal[m, which, t] = tile
                    nc.vector.tensor_scalar(out=tile[:], in0=ident[:], scalar1=token_gain(which, m, 1)[:, t:t + 1],
                                            scalar2=None, op0=ALU.mult)

        def gain_on_tensor(m, h, which):
            product_tile(m, h, which)
            for part in range(2):
                bank = psum.tile([P, PACK, H // 2], BF16, name="gain_bank", bufs=2)
                gain_banks[m, h, which, part] = bank
                for t in range(PACK):
                    nc.tensor.matmul(out=bank[:, t], lhsT=diagonal[m, which, t][:],
                                     rhs=raw[m, h][:, 1, t, part * H // 2:(part + 1) * H // 2], start=True, stop=True)

        def copy_gain_banks(m, h, which):
            target = products[m, h, which][:, 1]
            for part in range(2):
                bank = gain_banks[m, h, which, part]
                if which == U_GAIN:
                    nc.scalar.copy(
                        out=target[:, part * 2 * H:(part + 1) * 2 * H].rearrange("p (d t) -> p d t", t=PACK),
                        in_=bank[:].rearrange("p t d -> p d t"))
                else:
                    nc.scalar.copy(
                        out=target.rearrange("p (j part n t) -> p part j n t", j=NW, part=2, t=PACK)[:, part],
                        in_=bank[:].rearrange("p t (n j) -> p j n t", j=NW))

        def quantise_x(m, h, which):
            name = ("xu", "xv")[which]
            codes = pool.tile([P, NG, H], U32, name=name + "_codes", bufs=4, align_bytes=64)
            scales = pool.tile([P, NG, H], U8, name=name + "_scales", bufs=4, align_bytes=64)
            (xu_codes, xv_codes)[which][m, h] = (codes, scales)
            nc.vector.quantize_mx(
                out=codes[:].rearrange("p g d -> p (g d)").bitcast(E4M3X4),
                scales=scales[:].rearrange("p g d -> p (g d)"),
                in_=products[m, h, which][:].rearrange("p g d -> p (g d)"))


        def widen_tau(m, g):
            tile = pool.tile([P, PACK, F], BF16, name="tau_rows", bufs=2)
            tau_rows[m, g] = tile
            for t in range(PACK):
                nc.scalar.activation(out=tile[:, t], in_=tau_raw[m][:, g, t].bitcast(E4M3), func=COPY,
                                     scale=tau_scales[:, g, t:t + 1])

        def mix_tau(m, g):
            tile = pool.tile([P, F * PACK], BF16, name="tau_mixed", bufs=2, align_bytes=64)
            tau_mixed[m, g] = tile
            copy = nc.scalar.copy if (m, g) in TAU_MIX_ON_SCALAR else nc.vector.tensor_copy
            copy(out=tile[:].rearrange("p (c i t) -> p c t i", i=RUN, t=PACK),
                 in_=tau_rows[m, g][:].rearrange("p t (c i) -> p c t i", i=RUN))

        def quantise_tau(m, g):
            codes = pool.tile([P, F], U32, name="tau_codes", bufs=M * NG, align_bytes=64)
            scales = pool.tile([P, F], U8, name="tau_code_scales", bufs=M * NG, align_bytes=64)
            tau_codes[m, g] = (codes, scales)
            nc.vector.quantize_mx(out=codes[:].bitcast(E4M3X4), scales=scales[:], in_=tau_mixed[m, g][:])


        def gram(unit):
            m, h, g = unit
            gram_banks[unit] = []
            for t in range(PACK):
                bank = psum.tile([P, H], F32, name="gram_bank")
                gram_banks[unit].append(bank)
                for k in range(NG):
                    nc.tensor.matmul_mx(
                        out=bank[:],
                        lhsT=xv_codes[m, g][0][:, k, t * P:(t + 1) * P].bitcast(E4M3X4),
                        lhsT_scale=xv_codes[m, g][1][:, k, t * P:(t + 1) * P],
                        rhs=xu_codes[m, h][0][:, k].bitcast(E4M3X4),
                        rhs_scale=xu_codes[m, h][1][:, k],
                        start=(k == 0), stop=(k == NG - 1))

        def scale_gram(unit):
            m, h, g = unit
            rows = pool.tile([P, PACK, H], BF16, name="p_rows", bufs=2)
            p_rows[unit] = rows
            for t in range(PACK):
                windows = gram_banks[unit][t][:].rearrange("p (n j) -> p j n", j=NW)
                factor = c_scaled[:, NG * m + g, t:t + 1]
                spans = [(0, NW)]
                if h == g:
                    spans = [(lo, hi) for (lo, hi) in ((0, t), (t + 1, NW)) if hi > lo]
                    nc.vector.scalar_tensor_tensor(
                        out=rows[:, t, t * P:(t + 1) * P], in0=windows[:, t], scalar=factor, in1=boost[:],
                        op0=ALU.mult, op1=ALU.mult)
                for lo, hi in spans:
                    nc.scalar.activation(out=rows[:, t, lo * P:hi * P].rearrange("p (j n) -> p j n", n=P),
                                         in_=windows[:, lo:hi], func=COPY, scale=factor)

        def mix_p(unit):
            tile = pool.tile([P, H * PACK], BF16, name="p_mixed", bufs=2, align_bytes=64)
            p_mixed[unit] = tile
            copy = nc.scalar.copy if UNITS.index(unit) in P_MIX_ON_SCALAR else nc.vector.tensor_copy
            copy(out=tile[:].rearrange("p (c i t) -> p c t i", i=RUN, t=PACK),
                 in_=p_rows[unit][:].rearrange("p t (c i) -> p c t i", i=RUN))

        def quantise_p(unit):
            codes = pool.tile([P, H], U32, name="p_codes", bufs=len(UNITS), align_bytes=64)
            scales = pool.tile([P, H], U8, name="p_scales", bufs=len(UNITS), align_bytes=64)
            p_codes[unit] = (codes, scales)
            nc.vector.quantize_mx(out=codes[:].bitcast(E4M3X4), scales=scales[:], in_=p_mixed[unit][:])


        def apply(unit, pair):
            m, h, g = unit
            for j in (2 * pair, 2 * pair + 1):
                if (h, j) not in out_banks:
                    bank = psum.tile([P, F], F32, name="out_bank", tag=("out_bank", "gain_bank")[pair], bufs=2)
                    out_banks[h, j] = bank
                    out_passes[h, j] = 0
                done = out_passes[h, j]
                nc.tensor.matmul_mx(
                    out=out_banks[h, j][:],
                    lhsT=p_codes[unit][0][:, j * P:(j + 1) * P].bitcast(E4M3X4),
                    lhsT_scale=p_codes[unit][1][:, j * P:(j + 1) * P],
                    rhs=tau_codes[m, g][0][:].bitcast(E4M3X4),
                    rhs_scale=tau_codes[m, g][1][:],
                    start=(done == 0), stop=(done == M * NG - 1))
                out_passes[h, j] = done + 1

        def finish(h, j):
            result = pool.tile([P, F], F32, name="result", bufs=4)
            nc.vector.scalar_tensor_tensor(out=result[:], in0=out_banks[h, j][:], scalar=STEP, in1=w0_sb[:, h, j],
                                           op0=ALU.mult, op1=ALU.add)
            nc.sync.dma_start(out=out.rearrange("(h p j) f -> h j p f", h=HALVES, j=NW)[h, j], in_=result[:])


        make_identity(nc, ident[:])
        with tc.manual_schedule():
            load_x(0, 0, 0)
            load_gains(0, 1, u_first, v_first)
            load_x(0, 0, 1)
            load_x(0, 1, 0)
            load_x(0, 1, 1)
            nc.sync.dma_start(out=c_gain[:], in_=c.rearrange("m (g p t) -> p (m g) t", p=P, t=PACK))
            nc.sync.dma_start(out=tau_scales[:],
                              in_=tau_scale.rearrange("o (g p t) z -> p (o g) (t z)", p=P, t=PACK))
            load_tau(0)
            load_gains(1, M, u_rest, v_rest)
            for h in range(HALVES):
                for g in range(NG):
                    load_x(1, h, g)
            load_tau(1)
            load_x(2, 0, 0)
            load_x(2, 0, 1)
            nc.sync.dma_start(out=w0_sb[:].rearrange("p h j f -> p h (j f)"),
                              in_=w0.rearrange("(h p j) f -> p h (j f)", h=HALVES, j=NW))

            mix_x(nc.vector.tensor_copy, 0, 0, 0, H // 2)
            mix_x(nc.scalar.copy, 0, 0, H // 2, H)
            make_diagonals(0)
            for which in GAIN_ORDER[0]:
                gain_on_tensor(0, 0, which)
                copy_gain_banks(0, 0, which)
                gain_on_vector(0, 0, which)
            mix_x(nc.vector.tensor_copy, 0, 1)
            quantise_x(0, 0, U_GAIN)


        first, second = GAIN_ORDER[1]
        gain_on_vector(0, 1, first)
        quantise_x(0, 0, V_GAIN)
        gain_on_tensor(0, 1, first)
        copy_gain_banks(0, 1, first)
        nc.vector.tensor_scalar(out=c_scaled[:], in0=c_gain[:], scalar1=SHRINK / T, scalar2=None, op0=ALU.mult)
        nc.vector.tensor_scalar(out=boost[:], in0=ident[:], scalar1=0.25, scalar2=1.0, op0=ALU.mult, op1=ALU.add)
        gram(UNITS[0])
        gain_on_tensor(0, 1, second)
        copy_gain_banks(0, 1, second)
        make_diagonals(1)
        make_diagonals(2)

        for k in range(1, len(CHUNKS)):
            m, h = CHUNKS[k]
            first, second = GAIN_ORDER[h]
            ahead = CHUNKS[k + 1] if k + 1 < len(CHUNKS) else None
            units = [UNITS[i] for i in UNITS_BESIDE[k]]
            tau_group = divmod(k - 1, NG)
            if k == 2:
                load_x(2, 1, 0)
                load_x(2, 1, 1)
            gain_on_vector(m, h, second)
            scale_gram(units[0])
            if ahead:
                ahead_first, ahead_second = GAIN_ORDER[ahead[1]]
                gain_on_tensor(*ahead, ahead_first)
            if len(units) > 1:
                gram(units[1])
            quantise_x(m, h, first)
            if ahead:
                copy_gain_banks(*ahead, ahead_first)
            mix_p(units[0])
            quantise_x(m, h, second)
            quantise_p(units[0])
            if ahead:
                gain_on_tensor(*ahead, ahead_second)
                mix_x(nc.vector.tensor_copy, *ahead)
            if len(units) > 1:
                scale_gram(units[1])
            if ahead:
                gain_on_vector(*ahead, ahead_first)
            gram(UNITS[UNITS_BESIDE[k][-1] + 1])
            widen_tau(*tau_group)
            if ahead:
                copy_gain_banks(*ahead, ahead_second)
            if len(units) > 1:
                mix_p(units[1])
            mix_tau(*tau_group)
            if k == 3:
                load_tau(2)
            if len(units) > 1:
                quantise_p(units[1])
            quantise_tau(*tau_group)
            if k > 1:
                for i in UNITS_BESIDE[k - 1]:
                    if UNITS[i][1] == 0:
                        apply(UNITS[i], 0)
        widen_tau(M - 1, NG - 1)
        mix_tau(M - 1, NG - 1)
        quantise_tau(M - 1, NG - 1)

        for i in range(FIRST_TAIL_UNIT):
            if UNITS[i][1] == 0:
                apply(UNITS[i], 1)
                if i in UNITS_BESIDE[len(CHUNKS) - 1]:
                    apply(UNITS[i], 0)
        for i in range(FIRST_TAIL_UNIT, len(UNITS)):
            unit = UNITS[i]
            scale_gram(unit)
            if i < LAST_UNIT:
                gram(UNITS[i + 1])
            mix_p(unit)
            quantise_p(unit)
            if unit[1] == 0:
                apply(unit, 0)
                apply(unit, 1)
                for j in range(NW):
                    finish(0, j)
            if i == LAST_UNIT - 1:
                for earlier in UNITS[:LAST_UNIT]:
                    if earlier[1] == 1:
                        apply(earlier, 0)
                        apply(earlier, 1)
        apply(UNITS[LAST_UNIT], 0)
        apply(UNITS[LAST_UNIT], 1)
        for j in range(NW):
            finish(1, j)
